import numpy as np
import ml_dtypes


def mxq(x, axis, fmt="e4m3"):
    dtype, down = {"e4m3": (ml_dtypes.float8_e4m3fn, 7), "e5m2": (ml_dtypes.float8_e5m2, 14)}[fmt]
    v = np.moveaxis(np.asarray(x, np.float32).astype(ml_dtypes.bfloat16).astype(np.float64), axis, -1)
    blocks = v.reshape(v.shape[:-1] + (-1, 32))
    amax = np.abs(blocks).max(-1, keepdims=True)
    byte = np.maximum(np.where(amax > 0, np.frexp(amax)[1] - 1 + 127, 0) - down, 1)
    scale = np.exp2(byte - 127.0)
    codes = (blocks / scale).astype(np.float32).astype(dtype).astype(np.float64)
    return np.moveaxis((codes * scale).reshape(v.shape), -1, axis)


WIDE = False


def mx_kscale(k):
    if not WIDE:
        return np.ones(k)
    levels = np.array([10, -10, 5, -5, 0])
    if k % 512:
        return np.exp2(np.random.permutation(np.resize(levels, k // 32))).repeat(32)
    a = np.empty((k // 512, 16))
    for p in range(k // 512):
        a[p, :8] = np.random.permutation(np.resize(levels, 8))
        for g in range(8):
            far = levels[np.abs(levels - a[p, g]) >= 10]
            a[p, g + 8] = far[np.random.randint(len(far))]
    return np.exp2(a.ravel()).repeat(32)


def f64(x):
    return np.asarray(x).astype(np.float64)


def striped(idx):
    return np.tile(np.asarray(idx).reshape(-1, 16).T, (8, 1)).astype(np.uint16)


def unstriped(offs):
    return offs[:16].T.reshape(-1).astype(np.int64)


E2M1 = np.array([0.0, 0.5, 1.0, 1.5, 2.0, 3.0, 4.0, 6.0, -0.0, -0.5, -1.0, -1.5, -2.0, -3.0, -4.0, -6.0])


def pack_weight(w, fmt):
    k, n = w.shape
    w = f64(np.asarray(w, np.float32).astype(ml_dtypes.bfloat16)).reshape(k // 32, 32, n)
    amax = np.abs(w).max(1)
    if fmt == "e4m3":
        byte = np.frexp(amax)[1] - 1 + 127 - 7
    else:
        mant, ex = np.frexp(amax / 6.0)
        byte = np.where(mant > 0.5, ex, ex - 1) + 127
    byte = np.clip(np.where(amax > 0, byte, 1), 1, 254)
    scaled = (w * np.exp2(127.0 - byte)[:, None, :]).reshape(k, n).astype(np.float32)
    by_word = np.ascontiguousarray(scaled.reshape(k // 512, 128, 4, n).transpose(0, 1, 3, 2))
    if fmt == "e4m3":
        words = by_word.astype(ml_dtypes.float8_e4m3fn).view(np.uint8)
    else:
        c = by_word.astype(ml_dtypes.float4_e2m1fn).view(np.uint8) & 0xF
        words = (c[..., 0::2] | (c[..., 1::2] << 4)).reshape(k // 512, 128, 2 * n)
    return np.ascontiguousarray(words), np.ascontiguousarray(byte.astype(np.uint8).reshape(k // 512, 16, n))


def unpack_weight(words, scales, fmt):
    g, _, n = scales.shape
    words = np.ascontiguousarray(words).reshape(g, 128, n, -1)
    if fmt == "e4m3":
        vals = words.view(ml_dtypes.float8_e4m3fn).astype(np.float64)
    else:
        nib = np.empty((g, 128, n, 4), np.uint8)
        nib[..., 0::2] = words & 0xF
        nib[..., 1::2] = words >> 4
        vals = E2M1[nib]
    vals = vals * np.repeat(np.exp2(scales.astype(np.float64) - 127.0), 8, axis=1)[..., None]
    return vals.transpose(0, 1, 3, 2).reshape(g * 512, n)


B, N, T, D, NQ = 1, 512, 2048, 1024, 128


def setup_inputs():
    n = np.random.standard_normal
    idx = np.random.permutation(T)[:B * N]
    s = mx_kscale(D)[:, None]
    kp = pack_weight(n((D, T)) / s, "e2m1")
    return {
        "qT": (n((B, D, NQ)) * s * (1.00 / np.sqrt(D))).astype(np.float32),
        "k_words": np.ascontiguousarray(kp[0].reshape(1, 2, 128, T, 2).transpose(0, 2, 3, 1, 4)).reshape(1, 128, T, 4),
        "k_scales": kp[1],
        "offs": striped(idx),
    }


def reference(qT, k_words, k_scales, offs):
    idx = unstriped(offs)
    pick = lambda x, which: x[:, which].reshape(x.shape[0], B, -1).transpose(1, 0, 2)
    k = unpack_weight(k_words.reshape(1, 128, T, 2, 2).transpose(0, 3, 1, 2, 4).reshape(2, 128, 2 * T), k_scales, "e2m1")
    kg = pick(k, idx)
    qq = mxq(f64(qT), 1, "e4m3")
    a = qq.transpose(0, 2, 1) @ kg
    m = np.maximum(np.max(a, axis=-1, keepdims=True), 0.0)
    e = np.exp(a - m)
    y = e / (np.sum(e, axis=-1, keepdims=True) + np.exp(-m))
    return y

@@ -1,0 +1,101 @@
+from contextlib import ExitStack
+
+import concourse.mybir as mybir
+
+N, T, D, NQ = 512, 2048, 1024, 128
+FLOPS = 2 * D * NQ * N
+
+F32 = mybir.dt.float32
+BF16 = mybir.dt.bfloat16
+I32 = mybir.dt.int32
+U32 = mybir.dt.uint32
+U16 = mybir.dt.uint16
+U8 = mybir.dt.uint8
+FP8X4 = mybir.dt.float8_e4m3fn_x4
+FP4X4 = mybir.dt.float4_e2m1fn_x4
+ALU = mybir.AluOpType
+ACT = mybir.ActivationFunctionType
+
+P = 128
+PACK = 4
+K_PASS = P * PACK
+PASSES = D // K_PASS
+
+
+def tile_attend_nrm_off1_topk_kernel(tc, qT, k_words, k_scales, offs, out):
+    nc = tc.nc
+    with ExitStack() as ctx:
+        keep = ctx.enter_context(tc.tile_pool(name="keep", bufs=1))
+        psum = ctx.enter_context(tc.psum_pool(name="psum", bufs=1))
+
+        offsets = keep.tile([P, N // 16], U16, name="offsets")
+        nc.sync.dma_start(offsets[:], offs)
+
+        pool_scales = keep.tile([P, T // 4], I32, name="pool_scales", align_bytes=64)
+        nc.vector.memset(pool_scales[:], 0)
+        nc.scalar.dma_start(pool_scales[0:P:4, :], k_scales.rearrange("o f t -> (o f) t").bitcast(I32))
+
+        pool_words = keep.tile([P, T], I32, name="pool_words", align_bytes=64)
+        nc.sync.dma_start(pool_words[:], k_words[0].rearrange("p t b -> p (t b)").bitcast(I32))
+
+        q_raw = []
+        for o in range(PASSES):
+            raw = keep.tile([P, PACK, NQ], F32, name="q_raw%d" % o)
+            nc.sync.dma_start(raw[:], qT[0, o * K_PASS : (o + 1) * K_PASS, :].rearrange("(p j) w -> p j w", j=PACK))
+            q_raw.append(raw)
+
+        k_planes = []
+        for o in range(PASSES):
+            plane = keep.tile([P, N // 4], I32, name="k_plane%d" % o, align_bytes=64)
+            nc.vector.memset(plane[:], 0)
+            k_planes.append(plane)
+
+        zero = keep.tile([P, 1], F32, name="zero")
+        nc.vector.memset(zero[:], 0.0)
+        neg = keep.tile([P, N + 1], F32, name="neg")
+        nc.scalar.activation(neg[:, N : N + 1], zero[:], ACT.Copy)
+
+        got_scales = keep.tile([P, N], U8, name="got_scales", align_bytes=64)
+        nc.vector.tensor_copy(got_scales[:], pool_scales[:].bitcast(U8).indirect(offsets[:]))
+        for quad in range(4):
+            for o in range(PASSES):
+                first = 64 * o + 16 * quad
+                queue = nc.scalar if o == 0 else nc.sync
+                queue.dma_start(k_planes[o][32 * quad : 32 * quad + 4, :], got_scales[first : first + 16 : 4, :].bitcast(I32))
+
+        got_words = keep.tile([P, N], U32, name="got_words", align_bytes=64)
+        nc.vector.tensor_copy(got_words[:], pool_words[:].bitcast(U32).indirect(offsets[:]))
+        halves = got_words[:].bitcast(U16).rearrange("p (n o) -> p o n", o=PASSES)
+
+        scores = psum.tile([NQ, N], F32, name="scores")
+        for o in range(PASSES):
+            grouped = keep.tile([P, NQ, PACK], BF16, name="grouped%d" % o, align_bytes=64)
+            nc.scalar.copy(grouped[:], q_raw[o][:].rearrange("p j w -> p w j"))
+            k_codes = keep.tile([P, N], U16, name="k_codes%d" % o, align_bytes=64)
+            nc.vector.tensor_copy(k_codes[:], halves[:, o, :])
+            q_codes = keep.tile([P, NQ], U32, name="q_codes%d" % o, align_bytes=64)
+            q_plane = keep.tile([P, NQ], U8, name="q_plane%d" % o, align_bytes=64)
+            nc.vector.quantize_mx(out=q_codes[:].bitcast(FP8X4), scales=q_plane[:], in_=grouped[:].rearrange("p w j -> p (w j)"))
+            nc.tensor.matmul_mx(
+                out=scores[:],
+                lhsT=q_codes[:].bitcast(FP8X4),
+                lhsT_scale=q_plane[:],
+                rhs=k_codes[:].bitcast(FP4X4),
+                rhs_scale=k_planes[o][:].bitcast(U8),
+                start=(o == 0),
+                stop=(o == PASSES - 1),
+            )
+
+        neg_max = keep.tile([P, 1], F32, name="neg_max")
+        nc.vector.tensor_scalar(neg[:, :N], scores[:], -1.0, 0.0, ALU.mult, ALU.min, accum_out=neg_max[:])
+        e = keep.tile([P, N + 1], F32, name="e")
+        den = keep.tile([P, 1], F32, name="den")
+        nc.scalar.activation(e[:], neg[:], ACT.Exp, bias=neg_max[:], scale=-1.0, accum_out=den[:])
+        inv = keep.tile([P, 1], F32, name="inv")
+        nc.vector.reciprocal(inv[:], den[:])
+        half = N // 2
+        for h in range(2):
+            y = keep.tile([P, half], F32, name="y%d" % h)
+            nc.vector.tensor_scalar(y[:], e[:, h * half : (h + 1) * half], inv[:], None, ALU.mult)
+            queue = nc.sync if h == 0 else nc.scalar
+            queue.dma_start(out[0, :, h * half : (h + 1) * half], y[:])

@@ -32,8 +32,7 @@ def tile_attend_nrm_off1_topk_kernel(tc, qT, k_words, k_scales, offs, out):
         nc.sync.dma_start(offsets[:], offs)
 
         pool_scales = keep.tile([P, T // 4], I32, name="pool_scales", align_bytes=64)
-        nc.vector.memset(pool_scales[:], 0)
-        nc.scalar.dma_start(pool_scales[0:P:4, :], k_scales.rearrange("o f t -> (o f) t").bitcast(I32))
+        nc.scalar.dma_start(pool_scales[0:32, :], k_scales.rearrange("o f t -> (o f) t").bitcast(I32))
 
         pool_words = keep.tile([P, T], I32, name="pool_words", align_bytes=64)
         nc.sync.dma_start(pool_words[:], k_words[0].rearrange("p t b -> p (t b)").bitcast(I32))
@@ -44,24 +43,25 @@ def tile_attend_nrm_off1_topk_kernel(tc, qT, k_words, k_scales, offs, out):
             nc.sync.dma_start(raw[:], qT[0, o * K_PASS : (o + 1) * K_PASS, :].rearrange("(p j) w -> p j w", j=PACK))
             q_raw.append(raw)
 
-        k_planes = []
-        for o in range(PASSES):
-            plane = keep.tile([P, N // 4], I32, name="k_plane%d" % o, align_bytes=64)
-            nc.vector.memset(plane[:], 0)
-            k_planes.append(plane)
-
         zero = keep.tile([P, 1], F32, name="zero")
         nc.vector.memset(zero[:], 0.0)
+        nc.vector.memset(pool_scales[32:64, :], 0)
+        nc.vector.memset(pool_scales[64:P, :], 0)
+        k_planes = keep.tile([P, PASSES, N // 4], I32, name="k_planes", align_bytes=64)
+        nc.vector.memset(k_planes[:], 0)
+
         neg = keep.tile([P, N + 1], F32, name="neg")
         nc.scalar.activation(neg[:, N : N + 1], zero[:], ACT.Copy)
 
         got_scales = keep.tile([P, N], U8, name="got_scales", align_bytes=64)
         nc.vector.tensor_copy(got_scales[:], pool_scales[:].bitcast(U8).indirect(offsets[:]))
-        for quad in range(4):
-            for o in range(PASSES):
-                first = 64 * o + 16 * quad
-                queue = nc.scalar if o == 0 else nc.sync
-                queue.dma_start(k_planes[o][32 * quad : 32 * quad + 4, :], got_scales[first : first + 16 : 4, :].bitcast(I32))
+        for o in range(PASSES):
+            for quad in range(4):
+                first = 16 * o + 4 * quad
+                if first == 0:
+                    nc.vector.tensor_copy(k_planes[0:4, 0, :], got_scales[0:4, :].bitcast(I32))
+                    continue
+                nc.sync.dma_start(k_planes[32 * quad : 32 * quad + 4, o, :], got_scales[first : first + 4, :].bitcast(I32))
 
         got_words = keep.tile([P, N], U32, name="got_words", align_bytes=64)
         nc.vector.tensor_copy(got_words[:], pool_words[:].bitcast(U32).indirect(offsets[:]))
@@ -69,19 +69,22 @@ def tile_attend_nrm_off1_topk_kernel(tc, qT, k_words, k_scales, offs, out):
 
         scores = psum.tile([NQ, N], F32, name="scores")
         for o in range(PASSES):
-            grouped = keep.tile([P, NQ, PACK], BF16, name="grouped%d" % o, align_bytes=64)
-            nc.scalar.copy(grouped[:], q_raw[o][:].rearrange("p j w -> p w j"))
-            k_codes = keep.tile([P, N], U16, name="k_codes%d" % o, align_bytes=64)
-            nc.vector.tensor_copy(k_codes[:], halves[:, o, :])
+            grouped = keep.tile([P, NQ, PACK], BF16, name="grouped%d" % o, tag="slot%d" % o, align_bytes=64)
+            nc.scalar.copy(
+                grouped[:].rearrange("p (c i) j -> p c j i", i=4),
+                q_raw[o][:].rearrange("p j (c i) -> p c j i", i=4),
+            )
             q_codes = keep.tile([P, NQ], U32, name="q_codes%d" % o, align_bytes=64)
             q_plane = keep.tile([P, NQ], U8, name="q_plane%d" % o, align_bytes=64)
             nc.vector.quantize_mx(out=q_codes[:].bitcast(FP8X4), scales=q_plane[:], in_=grouped[:].rearrange("p w j -> p (w j)"))
+            k_codes = keep.tile([P, N], U16, name="k_codes%d" % o, tag="slot%d" % (2 - 2 * o), align_bytes=64)
+            nc.vector.tensor_copy(k_codes[:], halves[:, o, :])
             nc.tensor.matmul_mx(
                 out=scores[:],
                 lhsT=q_codes[:].bitcast(FP8X4),
                 lhsT_scale=q_plane[:],
                 rhs=k_codes[:].bitcast(FP4X4),
-                rhs_scale=k_planes[o][:].bitcast(U8),
+                rhs_scale=k_planes[:, o, :].bitcast(U8),
                 start=(o == 0),
                 stop=(o == PASSES - 1),
             )
@@ -93,9 +96,10 @@ def tile_attend_nrm_off1_topk_kernel(tc, qT, k_words, k_scales, offs, out):
         nc.scalar.activation(e[:], neg[:], ACT.Exp, bias=neg_max[:], scale=-1.0, accum_out=den[:])
         inv = keep.tile([P, 1], F32, name="inv")
         nc.vector.reciprocal(inv[:], den[:])
-        half = N // 2
-        for h in range(2):
-            y = keep.tile([P, half], F32, name="y%d" % h)
-            nc.vector.tensor_scalar(y[:], e[:, h * half : (h + 1) * half], inv[:], None, ALU.mult)
-            queue = nc.sync if h == 0 else nc.scalar
-            queue.dma_start(out[0, :, h * half : (h + 1) * half], y[:])
+        cut = 320
+        y_left = keep.tile([P, cut], F32, name="y_left")
+        nc.vector.tensor_scalar(y_left[:], e[:, :cut], inv[:], None, ALU.mult)
+        nc.sync.dma_start(out[0, :, :cut], y_left[:])
+        y_right = keep.tile([P, N - cut], F32, name="y_right")
+        nc.scalar.activation(y_right[:], e[:, cut:N], ACT.Copy, scale=inv[:])
+        nc.scalar.dma_start(out[0, :, cut:], y_right[:])

@@ -64,21 +64,25 @@ def tile_attend_nrm_off1_topk_kernel(tc, qT, k_words, k_scales, offs, out):
                 nc.sync.dma_start(k_planes[32 * quad : 32 * quad + 4, o, :], got_scales[first : first + 4, :].bitcast(I32))
 
         got_words = keep.tile([P, N], U32, name="got_words", align_bytes=64)
-        nc.vector.tensor_copy(got_words[:], pool_words[:].bitcast(U32).indirect(offsets[:]))
+        half = N // 2
+        for h in range(2):
+            listed = offsets[:, h * half // 16 : (h + 1) * half // 16]
+            nc.vector.tensor_copy(got_words[:, h * half : (h + 1) * half], pool_words[:].bitcast(U32).indirect(listed))
         halves = got_words[:].bitcast(U16).rearrange("p (n o) -> p o n", o=PASSES)
 
         scores = psum.tile([NQ, N], F32, name="scores")
         for o in range(PASSES):
             grouped = keep.tile([P, NQ, PACK], BF16, name="grouped%d" % o, tag="slot%d" % o, align_bytes=64)
-            nc.scalar.copy(
-                grouped[:].rearrange("p (c i) j -> p c j i", i=4),
-                q_raw[o][:].rearrange("p j (c i) -> p c j i", i=4),
-            )
+            nc.scalar.copy(grouped[:], q_raw[o][:].rearrange("p j w -> p w j"))
             q_codes = keep.tile([P, NQ], U32, name="q_codes%d" % o, align_bytes=64)
             q_plane = keep.tile([P, NQ], U8, name="q_plane%d" % o, align_bytes=64)
             nc.vector.quantize_mx(out=q_codes[:].bitcast(FP8X4), scales=q_plane[:], in_=grouped[:].rearrange("p w j -> p (w j)"))
             k_codes = keep.tile([P, N], U16, name="k_codes%d" % o, tag="slot%d" % (2 - 2 * o), align_bytes=64)
-            nc.vector.tensor_copy(k_codes[:], halves[:, o, :])
+            if o == 0:
+                for h in range(2):
+                    nc.vector.tensor_copy(k_codes[:, h * half : (h + 1) * half], halves[:, o, h * half : (h + 1) * half])
+            else:
+                nc.vector.tensor_copy(k_codes[:], halves[:, o, :])
             nc.tensor.matmul_mx(
                 out=scores[:],
                 lhsT=q_codes[:].bitcast(FP8X4),
@@ -96,7 +100,7 @@ def tile_attend_nrm_off1_topk_kernel(tc, qT, k_words, k_scales, offs, out):
         nc.scalar.activation(e[:], neg[:], ACT.Exp, bias=neg_max[:], scale=-1.0, accum_out=den[:])
         inv = keep.tile([P, 1], F32, name="inv")
         nc.vector.reciprocal(inv[:], den[:])
-        cut = 320
+        cut = 256
         y_left = keep.tile([P, cut], F32, name="y_left")
         nc.vector.tensor_scalar(y_left[:], e[:, :cut], inv[:], None, ALU.mult)
         nc.sync.dma_start(out[0, :, :cut], y_left[:])

@@ -32,7 +32,7 @@ def tile_attend_nrm_off1_topk_kernel(tc, qT, k_words, k_scales, offs, out):
         nc.sync.dma_start(offsets[:], offs)
 
         pool_scales = keep.tile([P, T // 4], I32, name="pool_scales", align_bytes=64)
-        nc.scalar.dma_start(pool_scales[0:32, :], k_scales.rearrange("o f t -> (o f) t").bitcast(I32))
+        nc.sync.dma_start(pool_scales[0:32, :], k_scales.rearrange("o f t -> (o f) t").bitcast(I32))
 
         pool_words = keep.tile([P, T], I32, name="pool_words", align_bytes=64)
         nc.sync.dma_start(pool_words[:], k_words[0].rearrange("p t b -> p (t b)").bitcast(I32))
@@ -61,7 +61,8 @@ def tile_attend_nrm_off1_topk_kernel(tc, qT, k_words, k_scales, offs, out):
                 if first == 0:
                     nc.vector.tensor_copy(k_planes[0:4, 0, :], got_scales[0:4, :].bitcast(I32))
                     continue
-                nc.sync.dma_start(k_planes[32 * quad : 32 * quad + 4, o, :], got_scales[first : first + 4, :].bitcast(I32))
+                queue = nc.scalar if o == 0 else nc.sync
+                queue.dma_start(k_planes[32 * quad : 32 * quad + 4, o, :], got_scales[first : first + 4, :].bitcast(I32))
 
         got_words = keep.tile([P, N], U32, name="got_words", align_bytes=64)
         half = N // 2

@@ -39,7 +39,7 @@ def tile_attend_nrm_off1_topk_kernel(tc, qT, k_words, k_scales, offs, out):
 
         q_raw = []
         for o in range(PASSES):
-            raw = keep.tile([P, PACK, NQ], F32, name="q_raw%d" % o)
+            raw = keep.tile([P, PACK, NQ], F32, name="q_raw%d" % o, tag="raw%d" % o, align_bytes=64)
             nc.sync.dma_start(raw[:], qT[0, o * K_PASS : (o + 1) * K_PASS, :].rearrange("(p j) w -> p j w", j=PACK))
             q_raw.append(raw)
 
@@ -73,12 +73,12 @@ def tile_attend_nrm_off1_topk_kernel(tc, qT, k_words, k_scales, offs, out):
 
         scores = psum.tile([NQ, N], F32, name="scores")
         for o in range(PASSES):
-            grouped = keep.tile([P, NQ, PACK], BF16, name="grouped%d" % o, tag="slot%d" % o, align_bytes=64)
-            nc.scalar.copy(grouped[:], q_raw[o][:].rearrange("p j w -> p w j"))
+            grouped = keep.tile([P, NQ, PACK], BF16, name="grouped%d" % o, align_bytes=64)
+            nc.scalar.copy(grouped[:].rearrange("p (c i) t -> p c t i", i=4), q_raw[o][:].rearrange("p t (c i) -> p c t i", i=4))
             q_codes = keep.tile([P, NQ], U32, name="q_codes%d" % o, align_bytes=64)
             q_plane = keep.tile([P, NQ], U8, name="q_plane%d" % o, align_bytes=64)
             nc.vector.quantize_mx(out=q_codes[:].bitcast(FP8X4), scales=q_plane[:], in_=grouped[:].rearrange("p w j -> p (w j)"))
-            k_codes = keep.tile([P, N], U16, name="k_codes%d" % o, tag="slot%d" % (2 - 2 * o), align_bytes=64)
+            k_codes = keep.tile([P, N], U16, name="k_codes%d" % o, tag="raw%d" % (2 - 2 * o), align_bytes=64)
             if o == 0:
                 for h in range(2):
                     nc.vector.tensor_copy(k_codes[:, h * half : (h + 1) * half], halves[:, o, h * half : (h + 1) * half])

@@ -64,47 +64,53 @@ def tile_attend_nrm_off1_topk_kernel(tc, qT, k_words, k_scales, offs, out):
                 queue = nc.scalar if o == 0 else nc.sync
                 queue.dma_start(k_planes[32 * quad : 32 * quad + 4, o, :], got_scales[first : first + 4, :].bitcast(I32))
 
+        half, quarter = N // 2, N // 4
         got_words = keep.tile([P, N], U32, name="got_words", align_bytes=64)
-        half = N // 2
         for h in range(2):
             listed = offsets[:, h * half // 16 : (h + 1) * half // 16]
             nc.vector.tensor_copy(got_words[:, h * half : (h + 1) * half], pool_words[:].bitcast(U32).indirect(listed))
         halves = got_words[:].bitcast(U16).rearrange("p (n o) -> p o n", o=PASSES)
 
-        scores = psum.tile([NQ, N], F32, name="scores")
+        scores = [psum.tile([NQ, quarter], F32, name="scores%d" % c) for c in range(4)]
+        first_codes = keep.tile([P, half], U16, name="first_codes", align_bytes=64)
+        later_codes = keep.tile([P, 3, half], U16, name="later_codes", tag="raw0", align_bytes=64)
         for o in range(PASSES):
             grouped = keep.tile([P, NQ, PACK], BF16, name="grouped%d" % o, align_bytes=64)
             nc.scalar.copy(grouped[:].rearrange("p (c i) t -> p c t i", i=4), q_raw[o][:].rearrange("p t (c i) -> p c t i", i=4))
             q_codes = keep.tile([P, NQ], U32, name="q_codes%d" % o, align_bytes=64)
             q_plane = keep.tile([P, NQ], U8, name="q_plane%d" % o, align_bytes=64)
             nc.vector.quantize_mx(out=q_codes[:].bitcast(FP8X4), scales=q_plane[:], in_=grouped[:].rearrange("p w j -> p (w j)"))
-            k_codes = keep.tile([P, N], U16, name="k_codes%d" % o, tag="raw%d" % (2 - 2 * o), align_bytes=64)
-            if o == 0:
-                for h in range(2):
-                    nc.vector.tensor_copy(k_codes[:, h * half : (h + 1) * half], halves[:, o, h * half : (h + 1) * half])
-            else:
-                nc.vector.tensor_copy(k_codes[:], halves[:, o, :])
-            nc.tensor.matmul_mx(
-                out=scores[:],
-                lhsT=q_codes[:].bitcast(FP8X4),
-                lhsT_scale=q_plane[:],
-                rhs=k_codes[:].bitcast(FP4X4),
-                rhs_scale=k_planes[:, o, :].bitcast(U8),
-                start=(o == 0),
-                stop=(o == PASSES - 1),
-            )
+            for h in range(2):
+                k_codes = first_codes[:] if o == 0 and h == 0 else later_codes[:, 2 * o + h - 1, :]
+                nc.vector.tensor_copy(k_codes, halves[:, o, h * half : (h + 1) * half])
+                for r in range(2):
+                    c = 2 * h + r
+                    nc.tensor.matmul_mx(
+                        out=scores[c][:],
+                        lhsT=q_codes[:].bitcast(FP8X4),
+                        lhsT_scale=q_plane[:],
+                        rhs=k_codes[:, r * quarter : (r + 1) * quarter].bitcast(FP4X4),
+                        rhs_scale=k_planes[:, o, :].bitcast(U8)[:, c * quarter : (c + 1) * quarter],
+                        start=(o == 0),
+                        stop=(o == PASSES - 1),
+                    )
 
+        neg_maxes = keep.tile([P, 4], F32, name="neg_maxes")
+        for c in range(3):
+            nc.vector.tensor_reduce(neg_maxes[:, c : c + 1], scores[c][:], mybir.AxisListType.X, ALU.max, negate=True)
+            nc.scalar.activation(neg[:, c * quarter : (c + 1) * quarter], scores[c][:], ACT.Copy, scale=-1.0)
+        nc.vector.tensor_scalar(neg[:, 3 * quarter : N], scores[3][:], -1.0, 0.0, ALU.mult, ALU.min, accum_out=neg_maxes[:, 3:4])
         neg_max = keep.tile([P, 1], F32, name="neg_max")
-        nc.vector.tensor_scalar(neg[:, :N], scores[:], -1.0, 0.0, ALU.mult, ALU.min, accum_out=neg_max[:])
+        nc.vector.tensor_reduce(neg_max[:], neg_maxes[:], mybir.AxisListType.X, ALU.min)
         e = keep.tile([P, N + 1], F32, name="e")
         den = keep.tile([P, 1], F32, name="den")
         nc.scalar.activation(e[:], neg[:], ACT.Exp, bias=neg_max[:], scale=-1.0, accum_out=den[:])
         inv = keep.tile([P, 1], F32, name="inv")
         nc.vector.reciprocal(inv[:], den[:])
-        cut = 256
+        cut = 192
         y_left = keep.tile([P, cut], F32, name="y_left")
         nc.vector.tensor_scalar(y_left[:], e[:, :cut], inv[:], None, ALU.mult)
         nc.sync.dma_start(out[0, :, :cut], y_left[:])
         y_right = keep.tile([P, N - cut], F32, name="y_right")
-        nc.scalar.activation(y_right[:], e[:, cut:N], ACT.Copy, scale=inv[:])
+        nc.vector.tensor_scalar(y_right[:], e[:, cut:N], inv[:], None, ALU.mult)
         nc.scalar.dma_start(out[0, :, cut:], y_right[:])

@@ -43,15 +43,15 @@ def tile_attend_nrm_off1_topk_kernel(tc, qT, k_words, k_scales, offs, out):
             nc.sync.dma_start(raw[:], qT[0, o * K_PASS : (o + 1) * K_PASS, :].rearrange("(p j) w -> p j w", j=PACK))
             q_raw.append(raw)
 
-        zero = keep.tile([P, 1], F32, name="zero")
-        nc.vector.memset(zero[:], 0.0)
+        neg_maxes = keep.tile([P, 5], F32, name="neg_maxes")
+        nc.vector.memset(neg_maxes[:, 4:5], 0.0)
         nc.vector.memset(pool_scales[32:64, :], 0)
         nc.vector.memset(pool_scales[64:P, :], 0)
         k_planes = keep.tile([P, PASSES, N // 4], I32, name="k_planes", align_bytes=64)
         nc.vector.memset(k_planes[:], 0)
 
-        neg = keep.tile([P, N + 1], F32, name="neg")
-        nc.scalar.activation(neg[:, N : N + 1], zero[:], ACT.Copy)
+        sums = keep.tile([P, 5], F32, name="sums")
+        nc.scalar.activation(sums[:, 4:5], neg_maxes[:, 4:5], ACT.Exp)
 
         got_scales = keep.tile([P, N], U8, name="got_scales", align_bytes=64)
         nc.vector.tensor_copy(got_scales[:], pool_scales[:].bitcast(U8).indirect(offsets[:]))
@@ -95,22 +95,29 @@ def tile_attend_nrm_off1_topk_kernel(tc, qT, k_words, k_scales, offs, out):
                         stop=(o == PASSES - 1),
                     )
 
-        neg_maxes = keep.tile([P, 4], F32, name="neg_maxes")
-        for c in range(3):
+        e = keep.tile([P, N], F32, name="e")
+        for c in range(4):
             nc.vector.tensor_reduce(neg_maxes[:, c : c + 1], scores[c][:], mybir.AxisListType.X, ALU.max, negate=True)
-            nc.scalar.activation(neg[:, c * quarter : (c + 1) * quarter], scores[c][:], ACT.Copy, scale=-1.0)
-        nc.vector.tensor_scalar(neg[:, 3 * quarter : N], scores[3][:], -1.0, 0.0, ALU.mult, ALU.min, accum_out=neg_maxes[:, 3:4])
+            nc.scalar.activation(
+                e[:, c * quarter : (c + 1) * quarter], scores[c][:], ACT.Exp, bias=neg_maxes[:, c : c + 1], accum_out=sums[:, c : c + 1]
+            )
         neg_max = keep.tile([P, 1], F32, name="neg_max")
         nc.vector.tensor_reduce(neg_max[:], neg_maxes[:], mybir.AxisListType.X, ALU.min)
-        e = keep.tile([P, N + 1], F32, name="e")
+        factors = keep.tile([P, 5], F32, name="factors")
+        nc.scalar.activation(factors[:], neg_maxes[:], ACT.Exp, bias=neg_max[:], scale=-1.0)
+        terms = keep.tile([P, 5], F32, name="terms")
         den = keep.tile([P, 1], F32, name="den")
-        nc.scalar.activation(e[:], neg[:], ACT.Exp, bias=neg_max[:], scale=-1.0, accum_out=den[:])
+        nc.vector.scalar_tensor_tensor(terms[:], factors[:], 1.0, sums[:], ALU.mult, ALU.mult, accum_out=den[:])
         inv = keep.tile([P, 1], F32, name="inv")
         nc.vector.reciprocal(inv[:], den[:])
+        scaled = keep.tile([P, N], F32, name="scaled")
+        for c in range(4):
+            cols = slice(c * quarter, (c + 1) * quarter)
+            nc.vector.tensor_scalar(scaled[:, cols], e[:, cols], factors[:, c : c + 1], None, ALU.mult)
         cut = 192
         y_left = keep.tile([P, cut], F32, name="y_left")
-        nc.vector.tensor_scalar(y_left[:], e[:, :cut], inv[:], None, ALU.mult)
+        nc.vector.tensor_scalar(y_left[:], scaled[:, :cut], inv[:], None, ALU.mult)
         nc.sync.dma_start(out[0, :, :cut], y_left[:])
         y_right = keep.tile([P, N - cut], F32, name="y_right")
-        nc.vector.tensor_scalar(y_right[:], e[:, cut:N], inv[:], None, ALU.mult)
+        nc.vector.tensor_scalar(y_right[:], scaled[:, cut:N], inv[:], None, ALU.mult)
         nc.scalar.dma_start(out[0, :, cut:], y_right[:])

@@ -73,7 +73,9 @@ def tile_attend_nrm_off1_topk_kernel(tc, qT, k_words, k_scales, offs, out):
 
         scores = [psum.tile([NQ, quarter], F32, name="scores%d" % c) for c in range(4)]
         first_codes = keep.tile([P, half], U16, name="first_codes", align_bytes=64)
-        later_codes = keep.tile([P, 3, half], U16, name="later_codes", tag="raw0", align_bytes=64)
+        later_codes = keep.tile([P, 2, half], U16, name="later_codes", tag="raw0", align_bytes=64)
+        last_codes = keep.tile([P, half], U16, name="last_codes", tag="raw1", align_bytes=64)
+        key_codes = [[first_codes[:], later_codes[:, 0, :]], [later_codes[:, 1, :], last_codes[:]]]
         for o in range(PASSES):
             grouped = keep.tile([P, NQ, PACK], BF16, name="grouped%d" % o, align_bytes=64)
             nc.scalar.copy(grouped[:].rearrange("p (c i) t -> p c t i", i=4), q_raw[o][:].rearrange("p t (c i) -> p c t i", i=4))
@@ -81,7 +83,7 @@ def tile_attend_nrm_off1_topk_kernel(tc, qT, k_words, k_scales, offs, out):
             q_plane = keep.tile([P, NQ], U8, name="q_plane%d" % o, align_bytes=64)
             nc.vector.quantize_mx(out=q_codes[:].bitcast(FP8X4), scales=q_plane[:], in_=grouped[:].rearrange("p w j -> p (w j)"))
             for h in range(2):
-                k_codes = first_codes[:] if o == 0 and h == 0 else later_codes[:, 2 * o + h - 1, :]
+                k_codes = key_codes[o][h]
                 nc.vector.tensor_copy(k_codes, halves[:, o, h * half : (h + 1) * half])
                 for r in range(2):
                     c = 2 * h + r
@@ -113,7 +115,10 @@ def tile_attend_nrm_off1_topk_kernel(tc, qT, k_words, k_scales, offs, out):
         scaled = keep.tile([P, N], F32, name="scaled")
         for c in range(4):
             cols = slice(c * quarter, (c + 1) * quarter)
-            nc.vector.tensor_scalar(scaled[:, cols], e[:, cols], factors[:, c : c + 1], None, ALU.mult)
+            if c < 2:
+                nc.vector.tensor_scalar(scaled[:, cols], e[:, cols], factors[:, c : c + 1], None, ALU.mult)
+            else:
+                nc.scalar.activation(scaled[:, cols], e[:, cols], ACT.Copy, scale=factors[:, c : c + 1])
         cut = 192
         y_left = keep.tile([P, cut], F32, name="y_left")
         nc.vector.tensor_scalar(y_left[:], scaled[:, :cut], inv[:], None, ALU.mult)

@@ -119,10 +119,6 @@ def tile_attend_nrm_off1_topk_kernel(tc, qT, k_words, k_scales, offs, out):
                 nc.vector.tensor_scalar(scaled[:, cols], e[:, cols], factors[:, c : c + 1], None, ALU.mult)
             else:
                 nc.scalar.activation(scaled[:, cols], e[:, cols], ACT.Copy, scale=factors[:, c : c + 1])
-        cut = 192
-        y_left = keep.tile([P, cut], F32, name="y_left")
-        nc.vector.tensor_scalar(y_left[:], scaled[:, :cut], inv[:], None, ALU.mult)
-        nc.sync.dma_start(out[0, :, :cut], y_left[:])
-        y_right = keep.tile([P, N - cut], F32, name="y_right")
-        nc.vector.tensor_scalar(y_right[:], scaled[:, cut:N], inv[:], None, ALU.mult)
-        nc.scalar.dma_start(out[0, :, cut:], y_right[:])
+        y = keep.tile([P, N], F32, name="y")
+        nc.vector.tensor_scalar(y[:], scaled[:], inv[:], None, ALU.mult)
+        nc.sync.dma_start(out[0], y[:])

@@ -78,7 +78,13 @@ def tile_attend_nrm_off1_topk_kernel(tc, qT, k_words, k_scales, offs, out):
         key_codes = [[first_codes[:], later_codes[:, 0, :]], [later_codes[:, 1, :], last_codes[:]]]
         for o in range(PASSES):
             grouped = keep.tile([P, NQ, PACK], BF16, name="grouped%d" % o, align_bytes=64)
-            nc.scalar.copy(grouped[:].rearrange("p (c i) t -> p c t i", i=4), q_raw[o][:].rearrange("p t (c i) -> p c t i", i=4))
+            rounded = grouped[:].rearrange("p (c i) t -> p c t i", i=4)
+            raw = q_raw[o][:].rearrange("p t (c i) -> p c t i", i=4)
+            if o == 0:
+                nc.scalar.copy(rounded, raw)
+            else:
+                nc.scalar.copy(rounded[:, :24], raw[:, :24])
+                nc.vector.tensor_copy(rounded[:, 24:], raw[:, 24:])
             q_codes = keep.tile([P, NQ], U32, name="q_codes%d" % o, align_bytes=64)
             q_plane = keep.tile([P, NQ], U8, name="q_plane%d" % o, align_bytes=64)
             nc.vector.quantize_mx(out=q_codes[:].bitcast(FP8X4), scales=q_plane[:], in_=grouped[:].rearrange("p w j -> p (w j)"))
@@ -120,5 +126,7 @@ def tile_attend_nrm_off1_topk_kernel(tc, qT, k_words, k_scales, offs, out):
             else:
                 nc.scalar.activation(scaled[:, cols], e[:, cols], ACT.Copy, scale=factors[:, c : c + 1])
         y = keep.tile([P, N], F32, name="y")
-        nc.vector.tensor_scalar(y[:], scaled[:], inv[:], None, ALU.mult)
+        cut = 352
+        nc.vector.tensor_scalar(y[:, :cut], scaled[:, :cut], inv[:], None, ALU.mult)
+        nc.scalar.activation(y[:, cut:], scaled[:, cut:], ACT.Copy, scale=inv[:])
         nc.sync.dma_start(out[0], y[:])

@@ -20,6 +20,10 @@ P = 128
 PACK = 4
 K_PASS = P * PACK
 PASSES = D // K_PASS
+BANKS = 4
+BANK = N // BANKS
+SCALAR_ROWS = (96, 112)
+VECTOR_COLUMNS = 352
 
 
 def tile_attend_nrm_off1_topk_kernel(tc, qT, k_words, k_scales, offs, out):
@@ -30,28 +34,24 @@ def tile_attend_nrm_off1_topk_kernel(tc, qT, k_words, k_scales, offs, out):
 
         offsets = keep.tile([P, N // 16], U16, name="offsets")
         nc.sync.dma_start(offsets[:], offs)
-
         pool_scales = keep.tile([P, T // 4], I32, name="pool_scales", align_bytes=64)
         nc.sync.dma_start(pool_scales[0:32, :], k_scales.rearrange("o f t -> (o f) t").bitcast(I32))
-
         pool_words = keep.tile([P, T], I32, name="pool_words", align_bytes=64)
         nc.sync.dma_start(pool_words[:], k_words[0].rearrange("p t b -> p (t b)").bitcast(I32))
-
         q_raw = []
         for o in range(PASSES):
             raw = keep.tile([P, PACK, NQ], F32, name="q_raw%d" % o, tag="raw%d" % o, align_bytes=64)
             nc.sync.dma_start(raw[:], qT[0, o * K_PASS : (o + 1) * K_PASS, :].rearrange("(p j) w -> p j w", j=PACK))
             q_raw.append(raw)
 
-        neg_maxes = keep.tile([P, 5], F32, name="neg_maxes")
-        nc.vector.memset(neg_maxes[:, 4:5], 0.0)
+        neg_maxes = keep.tile([P, BANKS + 1], F32, name="neg_maxes")
+        nc.vector.memset(neg_maxes[:, BANKS:], 0.0)
         nc.vector.memset(pool_scales[32:64, :], 0)
         nc.vector.memset(pool_scales[64:P, :], 0)
         k_planes = keep.tile([P, PASSES, N // 4], I32, name="k_planes", align_bytes=64)
         nc.vector.memset(k_planes[:], 0)
-
-        sums = keep.tile([P, 5], F32, name="sums")
-        nc.scalar.activation(sums[:, 4:5], neg_maxes[:, 4:5], ACT.Exp)
+        sums = keep.tile([P, BANKS + 1], F32, name="sums")
+        nc.scalar.activation(sums[:, BANKS:], neg_maxes[:, BANKS:], ACT.Exp)
 
         got_scales = keep.tile([P, N], U8, name="got_scales", align_bytes=64)
         nc.vector.tensor_copy(got_scales[:], pool_scales[:].bitcast(U8).indirect(offsets[:]))
@@ -64,69 +64,86 @@ def tile_attend_nrm_off1_topk_kernel(tc, qT, k_words, k_scales, offs, out):
                 queue = nc.scalar if o == 0 else nc.sync
                 queue.dma_start(k_planes[32 * quad : 32 * quad + 4, o, :], got_scales[first : first + 4, :].bitcast(I32))
 
-        half, quarter = N // 2, N // 4
         got_words = keep.tile([P, N], U32, name="got_words", align_bytes=64)
         for h in range(2):
-            listed = offsets[:, h * half // 16 : (h + 1) * half // 16]
-            nc.vector.tensor_copy(got_words[:, h * half : (h + 1) * half], pool_words[:].bitcast(U32).indirect(listed))
-        halves = got_words[:].bitcast(U16).rearrange("p (n o) -> p o n", o=PASSES)
+            listed = offsets[:, h * 16 : (h + 1) * 16]
+            nc.vector.tensor_copy(got_words[:, h * 256 : (h + 1) * 256], pool_words[:].bitcast(U32).indirect(listed))
+        by_pass = got_words[:].bitcast(U16).rearrange("p (n o) -> p o n", o=PASSES)
 
-        scores = [psum.tile([NQ, quarter], F32, name="scores%d" % c) for c in range(4)]
-        first_codes = keep.tile([P, half], U16, name="first_codes", align_bytes=64)
-        later_codes = keep.tile([P, 2, half], U16, name="later_codes", tag="raw0", align_bytes=64)
-        last_codes = keep.tile([P, half], U16, name="last_codes", tag="raw1", align_bytes=64)
-        key_codes = [[first_codes[:], later_codes[:, 0, :]], [later_codes[:, 1, :], last_codes[:]]]
-        for o in range(PASSES):
-            grouped = keep.tile([P, NQ, PACK], BF16, name="grouped%d" % o, align_bytes=64)
+        first_codes = keep.tile([P, BANK], U16, name="first_codes", align_bytes=64)
+        later_codes = keep.tile([P, 7 * BANK], U16, name="later_codes", tag="raw0", align_bytes=64)
+
+        def key_codes(o, bank, banks):
+            if o == 0 and bank == 0:
+                return first_codes[:]
+            start = (o * BANKS + bank - 1) * BANK
+            return later_codes[:, start : start + banks * BANK]
+
+        def split(o, bank, banks):
+            nc.vector.tensor_copy(key_codes(o, bank, banks), by_pass[:, o, bank * BANK : (bank + banks) * BANK])
+
+        def quantise(o):
+            grouped = keep.tile([P, NQ, PACK], BF16, name="grouped%d" % o, tag="grouped%d" % o, align_bytes=64)
+            rows = SCALAR_ROWS[o]
             rounded = grouped[:].rearrange("p (c i) t -> p c t i", i=4)
             raw = q_raw[o][:].rearrange("p t (c i) -> p c t i", i=4)
+            nc.scalar.copy(rounded[:, : rows // 4], raw[:, : rows // 4])
             if o == 0:
-                nc.scalar.copy(rounded, raw)
+                nc.gpsimd.tensor_scalar(
+                    grouped[:, rows:, :], q_raw[o][:].rearrange("p t w -> p w t")[:, rows:, :], 1.0, 0.0, ALU.mult, ALU.add
+                )
             else:
-                nc.scalar.copy(rounded[:, :24], raw[:, :24])
-                nc.vector.tensor_copy(rounded[:, 24:], raw[:, 24:])
-            q_codes = keep.tile([P, NQ], U32, name="q_codes%d" % o, align_bytes=64)
+                nc.vector.tensor_copy(rounded[:, rows // 4 :], raw[:, rows // 4 :])
+            q_codes = keep.tile([P, NQ], U32, name="q_codes%d" % o, tag="grouped0" if o else "q_codes0", align_bytes=64)
             q_plane = keep.tile([P, NQ], U8, name="q_plane%d" % o, align_bytes=64)
             nc.vector.quantize_mx(out=q_codes[:].bitcast(FP8X4), scales=q_plane[:], in_=grouped[:].rearrange("p w j -> p (w j)"))
-            for h in range(2):
-                k_codes = key_codes[o][h]
-                nc.vector.tensor_copy(k_codes, halves[:, o, h * half : (h + 1) * half])
-                for r in range(2):
-                    c = 2 * h + r
-                    nc.tensor.matmul_mx(
-                        out=scores[c][:],
-                        lhsT=q_codes[:].bitcast(FP8X4),
-                        lhsT_scale=q_plane[:],
-                        rhs=k_codes[:, r * quarter : (r + 1) * quarter].bitcast(FP4X4),
-                        rhs_scale=k_planes[:, o, :].bitcast(U8)[:, c * quarter : (c + 1) * quarter],
-                        start=(o == 0),
-                        stop=(o == PASSES - 1),
-                    )
+            return q_codes, q_plane
+
+        split(0, 0, 1)
+        queries = [quantise(0)]
+        split(0, 1, 1)
+        split(0, 2, 2)
+        split(1, 0, 2)
+        queries.append(quantise(1))
+        split(1, 2, 2)
+
+        scores = [psum.tile([NQ, BANK], F32, name="scores%d" % c) for c in range(BANKS)]
+        for o in range(PASSES):
+            q_codes, q_plane = queries[o]
+            for c in range(BANKS):
+                nc.tensor.matmul_mx(
+                    out=scores[c][:],
+                    lhsT=q_codes[:].bitcast(FP8X4),
+                    lhsT_scale=q_plane[:],
+                    rhs=key_codes(o, c, 1).bitcast(FP4X4),
+                    rhs_scale=k_planes[:, o, :].bitcast(U8)[:, c * BANK : (c + 1) * BANK],
+                    start=(o == 0),
+                    stop=(o == PASSES - 1),
+                )
 
         e = keep.tile([P, N], F32, name="e")
-        for c in range(4):
+        for c in range(BANKS):
             nc.vector.tensor_reduce(neg_maxes[:, c : c + 1], scores[c][:], mybir.AxisListType.X, ALU.max, negate=True)
             nc.scalar.activation(
-                e[:, c * quarter : (c + 1) * quarter], scores[c][:], ACT.Exp, bias=neg_maxes[:, c : c + 1], accum_out=sums[:, c : c + 1]
+                e[:, c * BANK : (c + 1) * BANK], scores[c][:], ACT.Exp, bias=neg_maxes[:, c : c + 1], accum_out=sums[:, c : c + 1]
             )
         neg_max = keep.tile([P, 1], F32, name="neg_max")
         nc.vector.tensor_reduce(neg_max[:], neg_maxes[:], mybir.AxisListType.X, ALU.min)
-        factors = keep.tile([P, 5], F32, name="factors")
+        factors = keep.tile([P, BANKS + 1], F32, name="factors")
         nc.scalar.activation(factors[:], neg_maxes[:], ACT.Exp, bias=neg_max[:], scale=-1.0)
-        terms = keep.tile([P, 5], F32, name="terms")
+        terms = keep.tile([P, BANKS + 1], F32, name="terms")
         den = keep.tile([P, 1], F32, name="den")
         nc.vector.scalar_tensor_tensor(terms[:], factors[:], 1.0, sums[:], ALU.mult, ALU.mult, accum_out=den[:])
         inv = keep.tile([P, 1], F32, name="inv")
         nc.vector.reciprocal(inv[:], den[:])
         scaled = keep.tile([P, N], F32, name="scaled")
-        for c in range(4):
-            cols = slice(c * quarter, (c + 1) * quarter)
+        for c in range(BANKS):
+            cols = slice(c * BANK, (c + 1) * BANK)
             if c < 2:
                 nc.vector.tensor_scalar(scaled[:, cols], e[:, cols], factors[:, c : c + 1], None, ALU.mult)
             else:
                 nc.scalar.activation(scaled[:, cols], e[:, cols], ACT.Copy, scale=factors[:, c : c + 1])
         y = keep.tile([P, N], F32, name="y")
-        cut = 352
-        nc.vector.tensor_scalar(y[:, :cut], scaled[:, :cut], inv[:], None, ALU.mult)
-        nc.scalar.activation(y[:, cut:], scaled[:, cut:], ACT.Copy, scale=inv[:])
+        nc.vector.tensor_scalar(y[:, :VECTOR_COLUMNS], scaled[:, :VECTOR_COLUMNS], inv[:], None, ALU.mult)
+        nc.scalar.activation(y[:, VECTOR_COLUMNS:], scaled[:, VECTOR_COLUMNS:], ACT.Copy, scale=inv[:])
         nc.sync.dma_start(out[0], y[:])

@@ -55,14 +55,16 @@ def tile_attend_nrm_off1_topk_kernel(tc, qT, k_words, k_scales, offs, out):
 
         got_scales = keep.tile([P, N], U8, name="got_scales", align_bytes=64)
         nc.vector.tensor_copy(got_scales[:], pool_scales[:].bitcast(U8).indirect(offsets[:]))
-        for o in range(PASSES):
-            for quad in range(4):
-                first = 16 * o + 4 * quad
-                if first == 0:
-                    nc.vector.tensor_copy(k_planes[0:4, 0, :], got_scales[0:4, :].bitcast(I32))
-                    continue
-                queue = nc.scalar if o == 0 else nc.sync
-                queue.dma_start(k_planes[32 * quad : 32 * quad + 4, o, :], got_scales[first : first + 4, :].bitcast(I32))
+        nc.vector.tensor_copy(k_planes[0:4, 0, :], got_scales[0:4, :].bitcast(I32))
+        early = N - BANK
+        moves = [(0, quad, 0, N) for quad in range(1, 4)] + [(1, 0, 0, N)]
+        moves += [(1, quad, 0, early) for quad in range(1, 4)] + [(1, quad, early, N) for quad in range(1, 4)]
+        for o, quad, lo, hi in moves:
+            first = 16 * o + 4 * quad
+            queue = nc.scalar if o == 0 else nc.sync
+            queue.dma_start(
+                k_planes[32 * quad : 32 * quad + 4, o, lo // 4 : hi // 4], got_scales[first : first + 4, lo:hi].bitcast(I32)
+            )
 
         got_words = keep.tile([P, N], U32, name="got_words", align_bytes=64)
         for h in range(2):

@@ -23,7 +23,7 @@ PASSES = D // K_PASS
 BANKS = 4
 BANK = N // BANKS
 SCALAR_ROWS = (96, 112)
-VECTOR_COLUMNS = 352
+VECTOR_COLUMNS = 304
 
 
 def tile_attend_nrm_off1_topk_kernel(tc, qT, k_words, k_scales, offs, out):
@@ -57,8 +57,8 @@ def tile_attend_nrm_off1_topk_kernel(tc, qT, k_words, k_scales, offs, out):
         nc.vector.tensor_copy(got_scales[:], pool_scales[:].bitcast(U8).indirect(offsets[:]))
         nc.vector.tensor_copy(k_planes[0:4, 0, :], got_scales[0:4, :].bitcast(I32))
         early = N - BANK
-        moves = [(0, quad, 0, N) for quad in range(1, 4)] + [(1, 0, 0, N)]
-        moves += [(1, quad, 0, early) for quad in range(1, 4)] + [(1, quad, early, N) for quad in range(1, 4)]
+        moves = [(0, quad, 0, N) for quad in range(1, 4)] + [(1, quad, 0, N) for quad in range(2)]
+        moves += [(1, quad, 0, early) for quad in range(2, 4)] + [(1, quad, early, N) for quad in range(2, 4)]
         for o, quad, lo, hi in moves:
             first = 16 * o + 4 * quad
             queue = nc.scalar if o == 0 else nc.sync

from contextlib import ExitStack

import concourse.mybir as mybir

N, T, D, NQ = 512, 2048, 1024, 128
FLOPS = 2 * D * NQ * N

F32 = mybir.dt.float32
BF16 = mybir.dt.bfloat16
I32 = mybir.dt.int32
U32 = mybir.dt.uint32
U16 = mybir.dt.uint16
U8 = mybir.dt.uint8
FP8X4 = mybir.dt.float8_e4m3fn_x4
FP4X4 = mybir.dt.float4_e2m1fn_x4
ALU = mybir.AluOpType
ACT = mybir.ActivationFunctionType

P = 128
PACK = 4
K_PASS = P * PACK
PASSES = D // K_PASS
BANKS = 4
BANK = N // BANKS
SCALAR_ROWS = (96, 112)
VECTOR_COLUMNS = 304


def tile_attend_nrm_off1_topk_kernel(tc, qT, k_words, k_scales, offs, out):
    nc = tc.nc
    with ExitStack() as ctx:
        keep = ctx.enter_context(tc.tile_pool(name="keep", bufs=1))
        psum = ctx.enter_context(tc.psum_pool(name="psum", bufs=1))

        offsets = keep.tile([P, N // 16], U16, name="offsets")
        nc.sync.dma_start(offsets[:], offs)
        pool_scales = keep.tile([P, T // 4], I32, name="pool_scales", align_bytes=64)
        nc.sync.dma_start(pool_scales[0:32, :], k_scales.rearrange("o f t -> (o f) t").bitcast(I32))
        pool_words = keep.tile([P, T], I32, name="pool_words", align_bytes=64)
        nc.sync.dma_start(pool_words[:], k_words[0].rearrange("p t b -> p (t b)").bitcast(I32))
        q_raw = []
        for o in range(PASSES):
            raw = keep.tile([P, PACK, NQ], F32, name="q_raw%d" % o, tag="raw%d" % o, align_bytes=64)
            nc.sync.dma_start(raw[:], qT[0, o * K_PASS : (o + 1) * K_PASS, :].rearrange("(p j) w -> p j w", j=PACK))
            q_raw.append(raw)

        neg_maxes = keep.tile([P, BANKS + 1], F32, name="neg_maxes")
        nc.vector.memset(neg_maxes[:, BANKS:], 0.0)
        nc.vector.memset(pool_scales[32:64, :], 0)
        nc.vector.memset(pool_scales[64:P, :], 0)
        k_planes = keep.tile([P, PASSES, N // 4], I32, name="k_planes", align_bytes=64)
        nc.vector.memset(k_planes[:], 0)
        sums = keep.tile([P, BANKS + 1], F32, name="sums")
        nc.scalar.activation(sums[:, BANKS:], neg_maxes[:, BANKS:], ACT.Exp)

        got_scales = keep.tile([P, N], U8, name="got_scales", align_bytes=64)
        nc.vector.tensor_copy(got_scales[:], pool_scales[:].bitcast(U8).indirect(offsets[:]))
        nc.vector.tensor_copy(k_planes[0:4, 0, :], got_scales[0:4, :].bitcast(I32))
        early = N - BANK
        moves = [(0, quad, 0, N) for quad in range(1, 4)] + [(1, quad, 0, N) for quad in range(2)]
        moves += [(1, quad, 0, early) for quad in range(2, 4)] + [(1, quad, early, N) for quad in range(2, 4)]
        for o, quad, lo, hi in moves:
            first = 16 * o + 4 * quad
            queue = nc.scalar if o == 0 else nc.sync
            queue.dma_start(
                k_planes[32 * quad : 32 * quad + 4, o, lo // 4 : hi // 4], got_scales[first : first + 4, lo:hi].bitcast(I32)
            )

        got_words = keep.tile([P, N], U32, name="got_words", align_bytes=64)
        for h in range(2):
            listed = offsets[:, h * 16 : (h + 1) * 16]
            nc.vector.tensor_copy(got_words[:, h * 256 : (h + 1) * 256], pool_words[:].bitcast(U32).indirect(listed))
        by_pass = got_words[:].bitcast(U16).rearrange("p (n o) -> p o n", o=PASSES)

        first_codes = keep.tile([P, BANK], U16, name="first_codes", align_bytes=64)
        later_codes = keep.tile([P, 7 * BANK], U16, name="later_codes", tag="raw0", align_bytes=64)

        def key_codes(o, bank, banks):
            if o == 0 and bank == 0:
                return first_codes[:]
            start = (o * BANKS + bank - 1) * BANK
            return later_codes[:, start : start + banks * BANK]

        def split(o, bank, banks):
            nc.vector.tensor_copy(key_codes(o, bank, banks), by_pass[:, o, bank * BANK : (bank + banks) * BANK])

        def quantise(o):
            grouped = keep.tile([P, NQ, PACK], BF16, name="grouped%d" % o, tag="grouped%d" % o, align_bytes=64)
            rows = SCALAR_ROWS[o]
            rounded = grouped[:].rearrange("p (c i) t -> p c t i", i=4)
            raw = q_raw[o][:].rearrange("p t (c i) -> p c t i", i=4)
            nc.scalar.copy(rounded[:, : rows // 4], raw[:, : rows // 4])
            if o == 0:
                nc.gpsimd.tensor_scalar(
                    grouped[:, rows:, :], q_raw[o][:].rearrange("p t w -> p w t")[:, rows:, :], 1.0, 0.0, ALU.mult, ALU.add
                )
            else:
                nc.vector.tensor_copy(rounded[:, rows // 4 :], raw[:, rows // 4 :])
            q_codes = keep.tile([P, NQ], U32, name="q_codes%d" % o, tag="grouped0" if o else "q_codes0", align_bytes=64)
            q_plane = keep.tile([P, NQ], U8, name="q_plane%d" % o, align_bytes=64)
            nc.vector.quantize_mx(out=q_codes[:].bitcast(FP8X4), scales=q_plane[:], in_=grouped[:].rearrange("p w j -> p (w j)"))
            return q_codes, q_plane

        split(0, 0, 1)
        queries = [quantise(0)]
        split(0, 1, 1)
        split(0, 2, 2)
        split(1, 0, 2)
        queries.append(quantise(1))
        split(1, 2, 2)

        scores = [psum.tile([NQ, BANK], F32, name="scores%d" % c) for c in range(BANKS)]
        for o in range(PASSES):
            q_codes, q_plane = queries[o]
            for c in range(BANKS):
                nc.tensor.matmul_mx(
                    out=scores[c][:],
                    lhsT=q_codes[:].bitcast(FP8X4),
                    lhsT_scale=q_plane[:],
                    rhs=key_codes(o, c, 1).bitcast(FP4X4),
                    rhs_scale=k_planes[:, o, :].bitcast(U8)[:, c * BANK : (c + 1) * BANK],
                    start=(o == 0),
                    stop=(o == PASSES - 1),
                )

        e = keep.tile([P, N], F32, name="e")
        for c in range(BANKS):
            nc.vector.tensor_reduce(neg_maxes[:, c : c + 1], scores[c][:], mybir.AxisListType.X, ALU.max, negate=True)
            nc.scalar.activation(
                e[:, c * BANK : (c + 1) * BANK], scores[c][:], ACT.Exp, bias=neg_maxes[:, c : c + 1], accum_out=sums[:, c : c + 1]
            )
        neg_max = keep.tile([P, 1], F32, name="neg_max")
        nc.vector.tensor_reduce(neg_max[:], neg_maxes[:], mybir.AxisListType.X, ALU.min)
        factors = keep.tile([P, BANKS + 1], F32, name="factors")
        nc.scalar.activation(factors[:], neg_maxes[:], ACT.Exp, bias=neg_max[:], scale=-1.0)
        terms = keep.tile([P, BANKS + 1], F32, name="terms")
        den = keep.tile([P, 1], F32, name="den")
        nc.vector.scalar_tensor_tensor(terms[:], factors[:], 1.0, sums[:], ALU.mult, ALU.mult, accum_out=den[:])
        inv = keep.tile([P, 1], F32, name="inv")
        nc.vector.reciprocal(inv[:], den[:])
        scaled = keep.tile([P, N], F32, name="scaled")
        for c in range(BANKS):
            cols = slice(c * BANK, (c + 1) * BANK)
            if c < 2:
                nc.vector.tensor_scalar(scaled[:, cols], e[:, cols], factors[:, c : c + 1], None, ALU.mult)
            else:
                nc.scalar.activation(scaled[:, cols], e[:, cols], ACT.Copy, scale=factors[:, c : c + 1])
        y = keep.tile([P, N], F32, name="y")
        nc.vector.tensor_scalar(y[:, :VECTOR_COLUMNS], scaled[:, :VECTOR_COLUMNS], inv[:], None, ALU.mult)
        nc.scalar.activation(y[:, VECTOR_COLUMNS:], scaled[:, VECTOR_COLUMNS:], ACT.Copy, scale=inv[:])
        nc.sync.dma_start(out[0], y[:])
